import numpy as np, ml_dtypes
CORES = [1,17,65,89,97,113]
N = 6
import mx_ref
NC, G = 128, 2
C = np.float32(0.000896)
A = np.float32(0.021)
BF = ml_dtypes.bfloat16
def cut(t, i, w=512):
    return t[:, w * i:w * i + w]
def tile(rs):
    return np.stack(rs, axis=2).reshape(128, -1).astype(BF)
def layer(w, X):
    out = []
    for i in range(G):
        for t in range(len(X)):
            p = mx_ref.matmul(mx_ref.quantize(cut(w, len(X) * i + t)), X[t])
            z = p if t == 0 else z + p
        out.append(z)
    return out
def silu(z):
    z = z.astype(np.float64); e = np.exp(-np.abs(z))
    return (z * np.where(z >= 0, 1, e) / (1 + e)).astype(np.float32)
def gate(U, V):
    return [(silu(s * u * A) * v) * C for u, v in zip(U, V) for s in (1, -1)]
def setup_inputs(rng):
    def f(*shape):
        return mx_ref.flush((rng.standard_normal(shape, dtype=np.float32) * np.exp2(rng.integers(-2, 3, shape[:-1] + (1,)))).astype(BF))
    return {"x": f(N, 128, 4 * NC), "u": f(N, 128, G * 512), "v": f(N, 128, G * 512), "w2": f(N, 128, 512)}
def setup_inputs_blocks(rng):
    d = setup_inputs(rng)
    for k in ("v", "w2"): d[k] = mx_ref.spread(d[k], rng, 4)
    for k in ("x", "u"): d[k] = mx_ref.spread(d[k], rng, 1)
    return d
def setup_inputs_wide(rng):
    d = setup_inputs(rng)
    for k in ("v", "w2"): d[k] = mx_ref.flush((d[k].astype(np.float32) * np.exp2(rng.integers(-5, 6, (N, 1, 1))).astype(np.float32)).astype(BF))
    return d
def setup_inputs_zeros(rng):
    d = setup_inputs(rng); v = d["x"].reshape(N, 128, -1, 4).copy()
    v[np.broadcast_to((rng.random((N, 1, v.shape[2], 1)) < 0.33), v.shape)] = 0
    d["x"] = v.reshape(d["x"].shape)
    return d
def reference(x, u, v, w2, own=None):
    h = np.zeros((N, 128, 4 * NC), BF)
    for j in range(N):
        X = [mx_ref.quantize(x[j])]
        h[j] = tile(gate(layer(u[j], X), layer(v[j], X)))
    use = h if own is None else own["h"]
    H = [mx_ref.quantize(use[j]) for j in range(N)]
    y = np.zeros((N, 128, N * NC), np.float32)
    for r in range(N):
        qw = mx_ref.quantize(w2[r])
        for j in range(N):
            y[r][:, NC * j:NC * j + NC] = mx_ref.matmul(qw, H[j])
    return {"h": h, "y": y}

import numpy as np
from concourse.bass import DstId, RemoteDMATransfer
from concourse.mybir import dt, AluOpType, ActivationFunctionType

N = 6
NC = 128
W = 512
A = float(np.float32(0.021))
C = float(np.float32(0.000896))

SCRATCH = {
    "xin": ("sbuf", [128, W], "bfloat16"),
    "uin": ("sbuf", [128, 2 * W], "bfloat16"),
    "vin": ("sbuf", [128, 2 * W], "bfloat16"),
    "win": ("sbuf", [128, W], "bfloat16"),
    "xq": ("sbuf", [128, NC], "float8_e4m3fn_x4"), "xs": ("sbuf", [128, NC], "uint8"),
    "uq": ("sbuf", [128, 2 * NC], "float8_e4m3fn_x4"), "us": ("sbuf", [128, 2 * NC], "uint8"),
    "vq": ("sbuf", [128, 2 * NC], "float8_e4m3fn_x4"), "vs": ("sbuf", [128, 2 * NC], "uint8"),
    "wq": ("sbuf", [128, NC], "float8_e4m3fn_x4"), "ws": ("sbuf", [128, NC], "uint8"),
    "pu0": ("psum", [128, 512], "float32"), "pu1": ("psum", [128, 512], "float32"),
    "pv0": ("psum", [128, 512], "float32"), "pv1": ("psum", [128, 512], "float32"),
    "py0": ("psum", [128, 512], "float32"), "py1": ("psum", [128, 512], "float32"),
    "py2": ("psum", [128, 512], "float32"), "py3": ("psum", [128, 512], "float32"),
    "sl": ("sbuf", [128, 4 * NC], "float32"),
    "tm": ("sbuf", [128, 4 * NC], "float32"),
    "ht": ("sbuf", [128, W], "bfloat16"),
    "hc": ("sbuf", [128, N * NC], "float8_e4m3fn_x4"),
    "hs": ("sbuf", [128, N * NC], "uint8"),
    "yb": ("sbuf", [128, N * NC], "float32"),
}
SEMAPHORES = (["lx", "lu0", "lu1", "lv0", "lv1", "lw", "qx", "qu0", "qu1", "qv0", "qv1", "qw", "qh",
               "mu0", "mu1", "mv0", "mv1", "rel", "sent", "sth"]
              + ["%s%d" % (p, i) for p in ("s", "t", "c") for i in range(4)]
              + ["%s%d" % (p, i) for p in ("a", "my", "cy", "st") for i in range(N)])


def bits(mask):
    return bin(mask).count("1")


def plan(T, topo, r):
    src = T.cores[r]
    n = len(T.cores)
    others = [(r + d) % n for d in range(1, n)]
    mine = [k for k in range(topo.CHIPS * topo.CORES_PER_CHIP)
            if topo.chip(k) == topo.chip(src) and T.rank_of(k) is None]
    able = [k for k in mine if all(topo.may_write(k, T.cores[j]) for j in others)]
    near = [k for k in able if topo.die(k) == topo.die(src)]
    far = [k for k in able if topo.die(k) != topo.die(src)]
    return [(near[0], "c", others[0:3]), (far[0], "p", others[0:3]),
            (far[1], "c", others[3:5]), (near[1], "p", others[3:5])]


def slot(T, kind, r):
    if kind == "c":
        return T.hc[:, NC * r:NC * r + NC].bitcast(dt.uint8)
    return T.hs[:, NC * r:NC * r + NC]


def relay(g, core, T, topo, r, kind, dsts):
    src = T.cores[r]
    mask = topo.mask(core, src)
    for j in dsts:
        mask &= topo.mask(core, T.cores[j])
    ids = []
    for j in dsts:
        rid, pid, _ = topo.addr(T.cores[j])
        ids.append(DstId(rid=rid, pnc=pid))
    g.wait_ge(T.sem.rel, bits(topo.mask(src, core)))
    g.remote_dma_fused([RemoteDMATransfer(dst_ids=ids, dma_engine_mask=mask, remote_sem=T.sem["a%d" % r],
                                          srcs=[slot(T, kind, r)], dsts=[slot(T, kind, r) for _ in dsts])],
                       local_sem=T.sem.sent)
    g.wait_ge(T.sem.sent, bits(mask))


def rank_program(g, core, T, topo):
    n = len(T.cores)
    rank = T.rank_of(core)
    if rank is None:
        for r in range(n):
            for helper, kind, dsts in plan(T, topo, r):
                if helper == core:
                    relay(g, core, T, topo, r, kind, dsts)
        return

    S = T.sem
    sy, sc, ve, pe = g.sync, g.scalar, g.vector, g.tensor
    Silu, Copy = ActivationFunctionType.Silu, ActivationFunctionType.Copy

    sy.dma_start(T.xin[:], T.x[:]).then_inc(S.lx, 16)
    sc.dma_start(T.uin[:, 0:W], T.u[:, 0:W]).then_inc(S.lu0, 16)
    sy.dma_start(T.uin[:, W:2 * W], T.u[:, W:2 * W]).then_inc(S.lu1, 16)
    sc.dma_start(T.vin[:, 0:W], T.v[:, 0:W]).then_inc(S.lv0, 16)
    sy.dma_start(T.vin[:, W:2 * W], T.v[:, W:2 * W]).then_inc(S.lv1, 16)
    sy.dma_start(T.win[:], T.w2[:]).then_inc(S.lw, 16)

    ve.wait_ge(S.lx, 16)
    ve.quantize_mx(T.xq[:], T.xs[:], T.xin[:]).then_inc(S.qx, 1)
    for name, q, s, t in (("u", T.uq, T.us, T.uin), ("v", T.vq, T.vs, T.vin)):
        for i in range(2):
            ve.wait_ge(S["l%s%d" % (name, i)], 16)
            ve.quantize_mx(q[:, NC * i:NC * i + NC], s[:, NC * i:NC * i + NC],
                           t[:, W * i:W * i + W]).then_inc(S["q%s%d" % (name, i)], 1)

    pe.wait_ge(S.qx, 1)
    for name, q, s in (("u", T.uq, T.us), ("v", T.vq, T.vs)):
        for i in range(2):
            pe.wait_ge(S["q%s%d" % (name, i)], 1)
            pe.matmul_mx(T["p%s%d" % (name, i)][:, 0:NC], q[:, NC * i:NC * i + NC], s[:, NC * i:NC * i + NC],
                         T.xq[:], T.xs[:], True, True).then_inc(S["m%s%d" % (name, i)], 1)

    def col(t, b):
        return t[:, NC * b:NC * b + NC]

    for b in range(4):
        if b % 2 == 0:
            sc.wait_ge(S["mu%d" % (b // 2)], 1)
        sc.activation(col(T.sl, b), T["pu%d" % (b // 2)][:, 0:NC], Silu,
                      scale=(A if b % 2 == 0 else -A)).then_inc(S["s%d" % b], 1)
    for b in range(4):
        if b % 2 == 0:
            ve.wait_ge(S["mv%d" % (b // 2)], 1)
        ve.wait_ge(S["s%d" % b], 1)
        ve.tensor_tensor(col(T.tm, b), col(T.sl, b), T["pv%d" % (b // 2)][:, 0:NC],
                         AluOpType.mult).then_inc(S["t%d" % b], 1)
    for b in range(3):
        sc.wait_ge(S["t%d" % b], 1)
        sc.activation(T.ht[:, b:W:4], col(T.tm, b), Copy, scale=C).then_inc(S["c%d" % b], 1)
    ve.wait_ge(S.t3, 1)
    ve.tensor_scalar(T.ht[:, 3:W:4], col(T.tm, 3), C, None, AluOpType.mult).then_inc(S.c3, 1)

    for b in range(4):
        ve.wait_ge(S["c%d" % b], 1)
    ve.quantize_mx(col(T.hc, rank), col(T.hs, rank), T.ht[:]).then_inc(S.qh, 1)
    ve.wait_ge(S.lw, 16)
    ve.quantize_mx(T.wq[:], T.ws[:], T.win[:]).then_inc(S.qw, 1)

    g.wait_ge(S.qh, 1)
    left = 0
    for helper, kind, dsts in plan(T, topo, rank):
        rid, pid, _ = topo.addr(helper)
        mask = topo.mask(core, helper)
        g.remote_dma(slot(T, kind, rank), slot(T, kind, rank), S.rel, S.sent, pid, rid, mask)
        left += bits(mask)

    sy.wait_ge(S.qh, 1)
    sy.wait_ge(S.sent, left)
    sy.dma_start(T.h[:], T.ht[:]).then_inc(S.sth, 16)

    order = [rank] + [(rank - d) % n for d in (1, 2, 4, 5, 3)]
    banks = [T.py0, T.py1, T.py2, T.py3, T.pu0, T.pu1]
    pe.wait_ge(S.qh, 1)
    pe.wait_ge(S.qw, 1)
    for i, j in enumerate(order):
        if j != rank:
            got = 0
            for helper, kind, dsts in plan(T, topo, j):
                if rank in dsts:
                    m = topo.mask(helper, T.cores[j])
                    for d in dsts:
                        m &= topo.mask(helper, T.cores[d])
                    got += bits(m)
            pe.wait_ge(S["a%d" % j], got)
        pe.matmul_mx(banks[i][:, 0:NC], T.wq[:], T.ws[:], col(T.hc, j), col(T.hs, j),
                     True, True).then_inc(S["my%d" % j], 1)
        if i % 2 == 0:
            ve.wait_ge(S["my%d" % j], 1)
            ve.tensor_copy(col(T.yb, j), banks[i][:, 0:NC]).then_inc(S["cy%d" % j], 1)
            q = sy
        else:
            sc.wait_ge(S["my%d" % j], 1)
            sc.activation(col(T.yb, j), banks[i][:, 0:NC], Copy).then_inc(S["cy%d" % j], 1)
            q = sc
        q.wait_ge(S["cy%d" % j], 1)
        q.dma_start(col(T.y, j), col(T.yb, j)).then_inc(S["st%d" % j], 16)
    sy.wait_ge(S.sth, 16)
    for i, j in enumerate(order):
        (sy if i % 2 == 0 else sc).wait_ge(S["st%d" % j], 16)
